import numpy as np, ml_dtypes
CORES = [2,3,42,43,82,83,122,123]
N = 8
import mx_ref
NC, WB = 512, 3
D = 2 * WB + 1
BF = ml_dtypes.bfloat16
def setup_inputs(rng):
    def f(*shape):
        return mx_ref.flush((rng.standard_normal(shape, dtype=np.float32) * np.exp2(rng.integers(-2, 3, shape[:-1] + (1,)))).astype(BF))
    return {"w": f(N, 128, D * 512), "x": f(N, 128, 4 * NC)}
def setup_inputs_blocks(rng):
    d = setup_inputs(rng)
    for k in ("w", "x"): d[k] = mx_ref.spread(d[k], rng, 2)
    return d
def setup_inputs_wide(rng):
    d = setup_inputs(rng)
    for k in ("w", "x"): d[k] = mx_ref.flush((d[k].astype(np.float32) * np.exp2(rng.integers(-8, 9, (N, 1, 1))).astype(np.float32)).astype(BF))
    return d
def setup_inputs_zeros(rng):
    d = setup_inputs(rng); v = d["x"].reshape(N, 128, -1, 4).copy()
    v[np.broadcast_to((rng.random((N, 1, v.shape[2], 1)) < 0.33), v.shape)] = 0
    d["x"] = v.reshape(d["x"].shape)
    return d
def reference(w, x):
    QX = [mx_ref.quantize(x[j]) for j in range(N)]
    y = np.zeros((N, 128, NC), np.float32)
    for r in range(N):
        for i in range(D):
            p = mx_ref.matmul(mx_ref.quantize(w[r][:, 512 * i:512 * i + 512]), QX[(r + i - WB) % N])
            y[r] = p if i == 0 else y[r] + p
    return {"y": y}

@@ -1,0 +1,212 @@
+from concourse.bass import DstId, RemoteDMATransfer
+from concourse.mybir import dt
+
+N, NC, WB = 8, 512, 3
+D = 2 * WB + 1
+BLOCKS = ((0, 256), (256, 512))
+SEQ = ("c0", "p", "c1")
+WHO = {"c0": 0, "p": 1, "c1": 1}
+SHARE = {"plane": 2, "near": 1, "far": 2}
+CHAIN = False
+WPARTS = ((0, 4), (4, 7))
+LANE_T0 = {"own": 0.0, "side": 1.0, "plane": 2.0, "near": 2.2, "far": 2.4}
+NB = len(BLOCKS)
+
+SCRATCH = {
+    "xb": ("sbuf", [128, 4 * NC], "bfloat16"),
+    "wb": ("sbuf", [128, 512 * D], "bfloat16"),
+    "wq": ("sbuf", [128, 128 * D], "float8_e4m3fn_x4"),
+    "ws": ("sbuf", [128, 128 * D], "uint8"),
+    "xq": ("sbuf", [128, NC * N], "float8_e4m3fn_x4"),
+    "xs": ("sbuf", [128, NC * N], "uint8"),
+    "ps": ("psum", [128, 512 * NB], "float32"),
+    "yb": ("sbuf", [128, NC], "float32"),
+}
+SEMAPHORES = (["sent", "st"]
+              + [n + str(b) for b in range(NB) for n in ("xl", "qx", "mm", "cp")]
+              + [n + str(k) for k in range(len(WPARTS)) for n in ("wl", "qw")]
+              + ["a%d_%s" % (j, p) for j in range(N) for p in SEQ])
+
+
+def _span(p):
+    if p[0] == "c":
+        return (True,) + BLOCKS[int(p[1:])]
+    return (False, 0, NC)
+
+
+def _bits(m):
+    return [e for e in range(m.bit_length()) if (m >> e) & 1]
+
+
+def _deal(engines, dsts):
+    q = len(engines) // len(dsts)
+    if q * len(dsts) == len(engines):
+        return [([d], engines[i * q:(i + 1) * q]) for i, d in enumerate(dsts)]
+    return [(list(dsts), list(engines))]
+
+
+def _plan(cores, topo):
+    ncore = topo.CHIPS * topo.CORES_PER_CHIP
+    chips = []
+    for c in cores:
+        if topo.chip(c) not in chips:
+            chips.append(topo.chip(c))
+    used = set(cores)
+
+    def alloc(chip, ok, prefer):
+        cand = [c for c in range(ncore) if topo.chip(c) == chip and c not in used and ok(c)]
+        best = [c for c in cand if prefer(c)] or cand
+        used.add(best[0])
+        return best[0]
+
+    kids, depth, lane = {}, {}, {}
+
+    def edge(a, b, j, p):
+        k = kids.setdefault((a, j, p), [])
+        if b not in k:
+            k.append(b)
+            depth[(b, j, p)] = depth[(a, j, p)] + 1
+
+    for j, s in enumerate(cores):
+        h = topo.chip(s)
+        for p in SEQ:
+            depth[(s, j, p)] = 0
+        lane[(s, j)] = "own"
+        at = chips.index(h)
+        turn = [c for c in cores if topo.chip(c) == h].index(s)
+        users = {c: [cores[r] for r in range(N) if r != j and (j - r + WB) % N < D and topo.chip(cores[r]) == c]
+                 for c in chips}
+        cross = 0
+        for c in chips[at + 1:] + chips[:at]:
+            us = users[c]
+            if not us:
+                continue
+            more = []
+            if topo.same_plane(h, c):
+                name = "plane"
+                via = [alloc(h, lambda x: all(topo.may_write(x, u) for u in us),
+                             lambda x: topo.die(x) != topo.die(s)) for _ in range(SHARE[name])]
+                more = users[h]
+            elif cross == 0:
+                cross = 1
+                name = "near"
+                if CHAIN:
+                    via = [us[turn % len(us)]]
+                else:
+                    via = [alloc(c, lambda x: True, lambda x: topo.die(x) == topo.die(us[0]))
+                           for _ in range(SHARE[name])]
+            else:
+                name = "far"
+                m = [x for x in range(topo.CHIPS) if topo.mates(x, c)][0]
+                via = [alloc(m, lambda x: all(topo.may_write(x, u) for u in us),
+                             lambda x: (topo.die(x) == topo.die(s)) == ((turn + n) % 2 == 0))
+                       for n in range(SHARE[name])]
+            for p in SEQ:
+                v = via[WHO[p] % len(via)]
+                edge(s, v, j, p)
+                for u in us + more:
+                    if u != v:
+                        edge(v, u, j, p)
+            for u in us:
+                lane[(u, j)] = name
+            for u in more:
+                lane[(u, j)] = "side"
+
+    calls, inc = {}, {}
+    for (a, j, p) in sorted(kids, key=lambda k: (depth[k], SEQ.index(k[2]), k[1])):
+        ds = kids[(a, j, p)]
+        off = [d for d in ds if topo.chip(d) != topo.chip(a)]
+        onc = [d for d in ds if topo.chip(d) == topo.chip(a)]
+        eoff = _bits(topo.mask(a, off[0])) if off else []
+        groups = _deal(eoff, off) if off else []
+        if onc:
+            groups += _deal([e for e in _bits(topo.mask(a, onc[0])) if e not in eoff], onc)
+        for dsts, es in groups:
+            for d in dsts:
+                inc[(d, j, p)] = len(es)
+        calls.setdefault(a, []).append((j, p, groups))
+    return calls, inc, lane
+
+
+def _view(T, j, p):
+    codes, lo, hi = _span(p)
+    if codes:
+        return T.xq[:, NC * j + lo:NC * j + hi].bitcast(dt.uint8)
+    return T.xs[:, NC * j + lo:NC * j + hi]
+
+
+def rank_program(g, core, T, topo):
+    cores = list(T.cores)
+    calls, inc, lane = _plan(cores, topo)
+    rank = T.rank_of(core)
+    sem = T.sem
+
+    if rank is not None:
+        q2 = (g.sync, g.scalar)
+        for b, (lo, hi) in enumerate(BLOCKS):
+            q2[b % 2].dma_start(T.xb[:, 4 * lo:4 * hi], T.x[:, 4 * lo:4 * hi]).then_inc(sem["xl%d" % b], 16)
+        for k, (lo, hi) in enumerate(WPARTS):
+            q2[k % 2].dma_start(T.wb[:, 512 * lo:512 * hi], T.w[:, 512 * lo:512 * hi]).then_inc(sem["wl%d" % k], 16)
+        for b, (lo, hi) in enumerate(BLOCKS):
+            g.vector.wait_ge(sem["xl%d" % b], 16)
+            g.vector.quantize_mx(T.xq[:, NC * rank + lo:NC * rank + hi], T.xs[:, NC * rank + lo:NC * rank + hi],
+                                 T.xb[:, 4 * lo:4 * hi]).then_inc(sem["qx%d" % b], 1)
+        for k, (lo, hi) in enumerate(WPARTS):
+            g.vector.wait_ge(sem["wl%d" % k], 16)
+            g.vector.quantize_mx(T.wq[:, 128 * lo:128 * hi], T.ws[:, 128 * lo:128 * hi],
+                                 T.wb[:, 512 * lo:512 * hi]).then_inc(sem["qw%d" % k], 1)
+
+    sent = 0
+    for j, p, groups in calls.get(core, []):
+        if cores[j] == core:
+            lo, hi = _span(p)[1:]
+            for b, (bl, bh) in enumerate(BLOCKS):
+                if bl < hi and lo < bh:
+                    g.wait_ge(sem["qx%d" % b], 1)
+        else:
+            g.wait_ge(sem["a%d_%s" % (j, p)], inc[(core, j, p)])
+        trs = []
+        for dsts, es in groups:
+            ids = [DstId(rid=topo.addr(d)[0], pnc=topo.addr(d)[1]) for d in dsts]
+            trs.append(RemoteDMATransfer(dst_ids=ids, dma_engine_mask=sum(1 << e for e in es),
+                                         remote_sem=sem["a%d_%s" % (j, p)],
+                                         srcs=[_view(T, j, p)], dsts=[_view(T, j, p) for _ in dsts]))
+            sent += len(es)
+        g.remote_dma_fused(trs, local_sem=sem.sent)
+    if sent:
+        g.wait_ge(sem.sent, sent)
+
+    if rank is None:
+        return
+
+    need = {b: ["c%d" % b, "p"] for b in range(NB)}
+    todo = sorted(((LANE_T0[lane[(core, (rank + i - WB) % N)]] + max(SEQ.index(p) for p in need[b]), i, b)
+                   for i in range(D) for b in range(NB)))
+    left = {b: D for b in range(NB)}
+    waited = set()
+
+    def twait(name, val):
+        if name not in waited:
+            waited.add(name)
+            g.tensor.wait_ge(sem[name], val)
+
+    for _, i, b in todo:
+        j = (rank + i - WB) % N
+        lo, hi = BLOCKS[b]
+        twait("qw%d" % [k for k, (a, z) in enumerate(WPARTS) if a <= i < z][0], 1)
+        if j == rank:
+            twait("qx%d" % b, 1)
+        else:
+            for p in need[b]:
+                twait("a%d_%s" % (j, p), inc[(core, j, p)])
+        mm = g.tensor.matmul_mx(T.ps[:, 512 * b:512 * b + hi - lo], T.wq[:, 128 * i:128 * i + 128],
+                                T.ws[:, 128 * i:128 * i + 128], T.xq[:, NC * j + lo:NC * j + hi],
+                                T.xs[:, NC * j + lo:NC * j + hi], left[b] == D, left[b] == 1)
+        left[b] -= 1
+        if left[b] == 0:
+            mm.then_inc(sem["mm%d" % b], 1)
+            g.vector.wait_ge(sem["mm%d" % b], 1)
+            g.vector.tensor_copy(T.yb[:, lo:hi], T.ps[:, 512 * b:512 * b + hi - lo]).then_inc(sem["cp%d" % b], 1)
+            g.sync.wait_ge(sem["cp%d" % b], 1)
+            g.sync.dma_start(T.y[:, lo:hi], T.yb[:, lo:hi]).then_inc(sem.st, 16)
+    g.sync.wait_ge(sem.st, 16 * NB)

@@ -3,13 +3,15 @@ from concourse.mybir import dt
 
 N, NC, WB = 8, 512, 3
 D = 2 * WB + 1
-BLOCKS = ((0, 256), (256, 512))
-SEQ = ("c0", "p", "c1")
-WHO = {"c0": 0, "p": 1, "c1": 1}
+BLOCKS = ((0, 128), (128, 384), (384, 512))
+SEQ = ("c0", "p", "c1", "c2")
+STRAIGHT = "d2"
+ORDER = SEQ + (STRAIGHT,)
+WHO = {"c0": 0, "p": 1, "c1": 0, "c2": 1}
 SHARE = {"plane": 2, "near": 1, "far": 2}
-CHAIN = False
+HAND_ENG, OUT_ENG, SIDE_ENG, FAN_ENG = 4, 4, 2, 16
 WPARTS = ((0, 4), (4, 7))
-LANE_T0 = {"own": 0.0, "side": 1.0, "plane": 2.0, "near": 2.2, "far": 2.4}
+LANE_T0 = {"own": 0.0, "side": 1.0, "near": 2.0, "far": 2.2, "plane": 2.4}
 NB = len(BLOCKS)
 
 SCRATCH = {
@@ -25,11 +27,11 @@ SCRATCH = {
 SEMAPHORES = (["sent", "st"]
               + [n + str(b) for b in range(NB) for n in ("xl", "qx", "mm", "cp")]
               + [n + str(k) for k in range(len(WPARTS)) for n in ("wl", "qw")]
-              + ["a%d_%s" % (j, p) for j in range(N) for p in SEQ])
+              + ["a%d_%s" % (j, p) for j in range(N) for p in ORDER])
 
 
 def _span(p):
-    if p[0] == "c":
+    if p[0] in "cd":
         return (True,) + BLOCKS[int(p[1:])]
     return (False, 0, NC)
 
@@ -90,11 +92,8 @@ def _plan(cores, topo):
             elif cross == 0:
                 cross = 1
                 name = "near"
-                if CHAIN:
-                    via = [us[turn % len(us)]]
-                else:
-                    via = [alloc(c, lambda x: True, lambda x: topo.die(x) == topo.die(us[0]))
-                           for _ in range(SHARE[name])]
+                via = [alloc(c, lambda x: True, lambda x: topo.die(x) == topo.die(us[0]))
+                       for _ in range(SHARE[name])]
             else:
                 name = "far"
                 m = [x for x in range(topo.CHIPS) if topo.mates(x, c)][0]
@@ -104,23 +103,31 @@ def _plan(cores, topo):
             for p in SEQ:
                 v = via[WHO[p] % len(via)]
                 edge(s, v, j, p)
-                for u in us + more:
-                    if u != v:
-                        edge(v, u, j, p)
+                if name == "plane" and turn == 0 and _span(p) == _span(STRAIGHT):
+                    depth[(s, j, STRAIGHT)] = 0
+                    for u in us:
+                        edge(s, u, j, STRAIGHT)
+                    us_p = []
+                else:
+                    us_p = us
+                for u in us_p + more:
+                    edge(v, u, j, p)
             for u in us:
                 lane[(u, j)] = name
             for u in more:
                 lane[(u, j)] = "side"
 
     calls, inc = {}, {}
-    for (a, j, p) in sorted(kids, key=lambda k: (depth[k], SEQ.index(k[2]), k[1])):
+    for (a, j, p) in sorted(kids, key=lambda k: (depth[k], ORDER.index(k[2]), k[1])):
         ds = kids[(a, j, p)]
         off = [d for d in ds if topo.chip(d) != topo.chip(a)]
         onc = [d for d in ds if topo.chip(d) == topo.chip(a)]
         eoff = _bits(topo.mask(a, off[0])) if off else []
-        groups = _deal(eoff, off) if off else []
+        groups = _deal(eoff[:OUT_ENG] if onc and a not in cores else eoff, off) if off else []
         if onc:
-            groups += _deal([e for e in _bits(topo.mask(a, onc[0])) if e not in eoff], onc)
+            eon = [e for e in _bits(topo.mask(a, onc[0])) if e not in eoff]
+            home = topo.chip(a) == topo.chip(cores[j])
+            groups += _deal(eon[:HAND_ENG if a in cores else SIDE_ENG if home else FAN_ENG], onc)
         for dsts, es in groups:
             for d in dsts:
                 inc[(d, j, p)] = len(es)
@@ -142,11 +149,10 @@ def rank_program(g, core, T, topo):
     sem = T.sem
 
     if rank is not None:
-        q2 = (g.sync, g.scalar)
         for b, (lo, hi) in enumerate(BLOCKS):
-            q2[b % 2].dma_start(T.xb[:, 4 * lo:4 * hi], T.x[:, 4 * lo:4 * hi]).then_inc(sem["xl%d" % b], 16)
+            g.sync.dma_start(T.xb[:, 4 * lo:4 * hi], T.x[:, 4 * lo:4 * hi]).then_inc(sem["xl%d" % b], 16)
         for k, (lo, hi) in enumerate(WPARTS):
-            q2[k % 2].dma_start(T.wb[:, 512 * lo:512 * hi], T.w[:, 512 * lo:512 * hi]).then_inc(sem["wl%d" % k], 16)
+            g.sync.dma_start(T.wb[:, 512 * lo:512 * hi], T.w[:, 512 * lo:512 * hi]).then_inc(sem["wl%d" % k], 16)
         for b, (lo, hi) in enumerate(BLOCKS):
             g.vector.wait_ge(sem["xl%d" % b], 16)
             g.vector.quantize_mx(T.xq[:, NC * rank + lo:NC * rank + hi], T.xs[:, NC * rank + lo:NC * rank + hi],
@@ -179,8 +185,10 @@ def rank_program(g, core, T, topo):
     if rank is None:
         return
 
-    need = {b: ["c%d" % b, "p"] for b in range(NB)}
-    todo = sorted(((LANE_T0[lane[(core, (rank + i - WB) % N)]] + max(SEQ.index(p) for p in need[b]), i, b)
+    def need(j, b):
+        return ["d%d" % b if (core, j, "d%d" % b) in inc else "c%d" % b, "p"]
+
+    todo = sorted(((LANE_T0[lane[(core, (rank + i - WB) % N)]] + max(SEQ.index(p) for p in ("c%d" % b, "p")), i, b)
                    for i in range(D) for b in range(NB)))
     left = {b: D for b in range(NB)}
     waited = set()
@@ -197,7 +205,7 @@ def rank_program(g, core, T, topo):
         if j == rank:
             twait("qx%d" % b, 1)
         else:
-            for p in need[b]:
+            for p in need(j, b):
                 twait("a%d_%s" % (j, p), inc[(core, j, p)])
         mm = g.tensor.matmul_mx(T.ps[:, 512 * b:512 * b + hi - lo], T.wq[:, 128 * i:128 * i + 128],
                                 T.ws[:, 128 * i:128 * i + 128], T.xq[:, NC * j + lo:NC * j + hi],
@@ -207,6 +215,6 @@ def rank_program(g, core, T, topo):
             mm.then_inc(sem["mm%d" % b], 1)
             g.vector.wait_ge(sem["mm%d" % b], 1)
             g.vector.tensor_copy(T.yb[:, lo:hi], T.ps[:, 512 * b:512 * b + hi - lo]).then_inc(sem["cp%d" % b], 1)
-            g.sync.wait_ge(sem["cp%d" % b], 1)
-            g.sync.dma_start(T.y[:, lo:hi], T.yb[:, lo:hi]).then_inc(sem.st, 16)
-    g.sync.wait_ge(sem.st, 16 * NB)
+            g.scalar.wait_ge(sem["cp%d" % b], 1)
+            g.scalar.dma_start(T.y[:, lo:hi], T.yb[:, lo:hi]).then_inc(sem.st, 16)
+    g.scalar.wait_ge(sem.st, 16 * NB)

from concourse.bass import DstId, RemoteDMATransfer
from concourse.mybir import dt

N, NC, WB = 8, 512, 3
D = 2 * WB + 1
BLOCKS = ((0, 128), (128, 384), (384, 512))
SEQ = ("c0", "p", "c1", "c2")
STRAIGHT = "d2"
ORDER = SEQ + (STRAIGHT,)
WHO = {"c0": 0, "p": 1, "c1": 0, "c2": 1}
SHARE = {"plane": 2, "near": 1, "far": 2}
HAND_ENG, OUT_ENG, SIDE_ENG, FAN_ENG = 4, 4, 2, 16
WPARTS = ((0, 4), (4, 7))
LANE_T0 = {"own": 0.0, "side": 1.0, "near": 2.0, "far": 2.2, "plane": 2.4}
NB = len(BLOCKS)

SCRATCH = {
    "xb": ("sbuf", [128, 4 * NC], "bfloat16"),
    "wb": ("sbuf", [128, 512 * D], "bfloat16"),
    "wq": ("sbuf", [128, 128 * D], "float8_e4m3fn_x4"),
    "ws": ("sbuf", [128, 128 * D], "uint8"),
    "xq": ("sbuf", [128, NC * N], "float8_e4m3fn_x4"),
    "xs": ("sbuf", [128, NC * N], "uint8"),
    "ps": ("psum", [128, 512 * NB], "float32"),
    "yb": ("sbuf", [128, NC], "float32"),
}
SEMAPHORES = (["sent", "st"]
              + [n + str(b) for b in range(NB) for n in ("xl", "qx", "mm", "cp")]
              + [n + str(k) for k in range(len(WPARTS)) for n in ("wl", "qw")]
              + ["a%d_%s" % (j, p) for j in range(N) for p in ORDER])


def _span(p):
    if p[0] in "cd":
        return (True,) + BLOCKS[int(p[1:])]
    return (False, 0, NC)


def _bits(m):
    return [e for e in range(m.bit_length()) if (m >> e) & 1]


def _deal(engines, dsts):
    q = len(engines) // len(dsts)
    if q * len(dsts) == len(engines):
        return [([d], engines[i * q:(i + 1) * q]) for i, d in enumerate(dsts)]
    return [(list(dsts), list(engines))]


def _plan(cores, topo):
    ncore = topo.CHIPS * topo.CORES_PER_CHIP
    chips = []
    for c in cores:
        if topo.chip(c) not in chips:
            chips.append(topo.chip(c))
    used = set(cores)

    def alloc(chip, ok, prefer):
        cand = [c for c in range(ncore) if topo.chip(c) == chip and c not in used and ok(c)]
        best = [c for c in cand if prefer(c)] or cand
        used.add(best[0])
        return best[0]

    kids, depth, lane = {}, {}, {}

    def edge(a, b, j, p):
        k = kids.setdefault((a, j, p), [])
        if b not in k:
            k.append(b)
            depth[(b, j, p)] = depth[(a, j, p)] + 1

    for j, s in enumerate(cores):
        h = topo.chip(s)
        for p in SEQ:
            depth[(s, j, p)] = 0
        lane[(s, j)] = "own"
        at = chips.index(h)
        turn = [c for c in cores if topo.chip(c) == h].index(s)
        users = {c: [cores[r] for r in range(N) if r != j and (j - r + WB) % N < D and topo.chip(cores[r]) == c]
                 for c in chips}
        cross = 0
        for c in chips[at + 1:] + chips[:at]:
            us = users[c]
            if not us:
                continue
            more = []
            if topo.same_plane(h, c):
                name = "plane"
                via = [alloc(h, lambda x: all(topo.may_write(x, u) for u in us),
                             lambda x: topo.die(x) != topo.die(s)) for _ in range(SHARE[name])]
                more = users[h]
            elif cross == 0:
                cross = 1
                name = "near"
                via = [alloc(c, lambda x: True, lambda x: topo.die(x) == topo.die(us[0]))
                       for _ in range(SHARE[name])]
            else:
                name = "far"
                m = [x for x in range(topo.CHIPS) if topo.mates(x, c)][0]
                via = [alloc(m, lambda x: all(topo.may_write(x, u) for u in us),
                             lambda x: (topo.die(x) == topo.die(s)) == ((turn + n) % 2 == 0))
                       for n in range(SHARE[name])]
            for p in SEQ:
                v = via[WHO[p] % len(via)]
                edge(s, v, j, p)
                if name == "plane" and turn == 0 and _span(p) == _span(STRAIGHT):
                    depth[(s, j, STRAIGHT)] = 0
                    for u in us:
                        edge(s, u, j, STRAIGHT)
                    us_p = []
                else:
                    us_p = us
                for u in us_p + more:
                    edge(v, u, j, p)
            for u in us:
                lane[(u, j)] = name
            for u in more:
                lane[(u, j)] = "side"

    calls, inc = {}, {}
    for (a, j, p) in sorted(kids, key=lambda k: (depth[k], ORDER.index(k[2]), k[1])):
        ds = kids[(a, j, p)]
        off = [d for d in ds if topo.chip(d) != topo.chip(a)]
        onc = [d for d in ds if topo.chip(d) == topo.chip(a)]
        eoff = _bits(topo.mask(a, off[0])) if off else []
        groups = _deal(eoff[:OUT_ENG] if onc and a not in cores else eoff, off) if off else []
        if onc:
            eon = [e for e in _bits(topo.mask(a, onc[0])) if e not in eoff]
            home = topo.chip(a) == topo.chip(cores[j])
            groups += _deal(eon[:HAND_ENG if a in cores else SIDE_ENG if home else FAN_ENG], onc)
        for dsts, es in groups:
            for d in dsts:
                inc[(d, j, p)] = len(es)
        calls.setdefault(a, []).append((j, p, groups))
    return calls, inc, lane


def _view(T, j, p):
    codes, lo, hi = _span(p)
    if codes:
        return T.xq[:, NC * j + lo:NC * j + hi].bitcast(dt.uint8)
    return T.xs[:, NC * j + lo:NC * j + hi]


def rank_program(g, core, T, topo):
    cores = list(T.cores)
    calls, inc, lane = _plan(cores, topo)
    rank = T.rank_of(core)
    sem = T.sem

    if rank is not None:
        for b, (lo, hi) in enumerate(BLOCKS):
            g.sync.dma_start(T.xb[:, 4 * lo:4 * hi], T.x[:, 4 * lo:4 * hi]).then_inc(sem["xl%d" % b], 16)
        for k, (lo, hi) in enumerate(WPARTS):
            g.sync.dma_start(T.wb[:, 512 * lo:512 * hi], T.w[:, 512 * lo:512 * hi]).then_inc(sem["wl%d" % k], 16)
        for b, (lo, hi) in enumerate(BLOCKS):
            g.vector.wait_ge(sem["xl%d" % b], 16)
            g.vector.quantize_mx(T.xq[:, NC * rank + lo:NC * rank + hi], T.xs[:, NC * rank + lo:NC * rank + hi],
                                 T.xb[:, 4 * lo:4 * hi]).then_inc(sem["qx%d" % b], 1)
        for k, (lo, hi) in enumerate(WPARTS):
            g.vector.wait_ge(sem["wl%d" % k], 16)
            g.vector.quantize_mx(T.wq[:, 128 * lo:128 * hi], T.ws[:, 128 * lo:128 * hi],
                                 T.wb[:, 512 * lo:512 * hi]).then_inc(sem["qw%d" % k], 1)

    sent = 0
    for j, p, groups in calls.get(core, []):
        if cores[j] == core:
            lo, hi = _span(p)[1:]
            for b, (bl, bh) in enumerate(BLOCKS):
                if bl < hi and lo < bh:
                    g.wait_ge(sem["qx%d" % b], 1)
        else:
            g.wait_ge(sem["a%d_%s" % (j, p)], inc[(core, j, p)])
        trs = []
        for dsts, es in groups:
            ids = [DstId(rid=topo.addr(d)[0], pnc=topo.addr(d)[1]) for d in dsts]
            trs.append(RemoteDMATransfer(dst_ids=ids, dma_engine_mask=sum(1 << e for e in es),
                                         remote_sem=sem["a%d_%s" % (j, p)],
                                         srcs=[_view(T, j, p)], dsts=[_view(T, j, p) for _ in dsts]))
            sent += len(es)
        g.remote_dma_fused(trs, local_sem=sem.sent)
    if sent:
        g.wait_ge(sem.sent, sent)

    if rank is None:
        return

    def need(j, b):
        return ["d%d" % b if (core, j, "d%d" % b) in inc else "c%d" % b, "p"]

    todo = sorted(((LANE_T0[lane[(core, (rank + i - WB) % N)]] + max(SEQ.index(p) for p in ("c%d" % b, "p")), i, b)
                   for i in range(D) for b in range(NB)))
    left = {b: D for b in range(NB)}
    waited = set()

    def twait(name, val):
        if name not in waited:
            waited.add(name)
            g.tensor.wait_ge(sem[name], val)

    for _, i, b in todo:
        j = (rank + i - WB) % N
        lo, hi = BLOCKS[b]
        twait("qw%d" % [k for k, (a, z) in enumerate(WPARTS) if a <= i < z][0], 1)
        if j == rank:
            twait("qx%d" % b, 1)
        else:
            for p in need(j, b):
                twait("a%d_%s" % (j, p), inc[(core, j, p)])
        mm = g.tensor.matmul_mx(T.ps[:, 512 * b:512 * b + hi - lo], T.wq[:, 128 * i:128 * i + 128],
                                T.ws[:, 128 * i:128 * i + 128], T.xq[:, NC * j + lo:NC * j + hi],
                                T.xs[:, NC * j + lo:NC * j + hi], left[b] == D, left[b] == 1)
        left[b] -= 1
        if left[b] == 0:
            mm.then_inc(sem["mm%d" % b], 1)
            g.vector.wait_ge(sem["mm%d" % b], 1)
            g.vector.tensor_copy(T.yb[:, lo:hi], T.ps[:, 512 * b:512 * b + hi - lo]).then_inc(sem["cp%d" % b], 1)
            g.scalar.wait_ge(sem["cp%d" % b], 1)
            g.scalar.dma_start(T.y[:, lo:hi], T.yb[:, lo:hi]).then_inc(sem.st, 16)
    g.scalar.wait_ge(sem.st, 16 * NB)
